import numpy as np
import ml_dtypes


def mxq(x, axis, fmt="e4m3"):
    dtype, down = {"e4m3": (ml_dtypes.float8_e4m3fn, 7), "e5m2": (ml_dtypes.float8_e5m2, 14)}[fmt]
    v = np.moveaxis(np.asarray(x, np.float32).astype(ml_dtypes.bfloat16).astype(np.float64), axis, -1)
    blocks = v.reshape(v.shape[:-1] + (-1, 32))
    amax = np.abs(blocks).max(-1, keepdims=True)
    byte = np.maximum(np.where(amax > 0, np.frexp(amax)[1] - 1 + 127, 0) - down, 1)
    scale = np.exp2(byte - 127.0)
    codes = (blocks / scale).astype(np.float32).astype(dtype).astype(np.float64)
    return np.moveaxis((codes * scale).reshape(v.shape), -1, axis)


WIDE = False


def mx_kscale(k):
    if not WIDE:
        return np.ones(k)
    levels = np.array([10, -10, 5, -5, 0])
    if k % 512:
        return np.exp2(np.random.permutation(np.resize(levels, k // 32))).repeat(32)
    a = np.empty((k // 512, 16))
    for p in range(k // 512):
        a[p, :8] = np.random.permutation(np.resize(levels, 8))
        for g in range(8):
            far = levels[np.abs(levels - a[p, g]) >= 10]
            a[p, g + 8] = far[np.random.randint(len(far))]
    return np.exp2(a.ravel()).repeat(32)


def f64(x):
    return np.asarray(x).astype(np.float64)


def striped(idx):
    return np.tile(idx.reshape(-1, 16).T, (8, 1)).astype(np.uint16)


def unstriped(offs):
    return offs[:16].T.reshape(-1).astype(np.int64)


def striped8(idx):
    return np.concatenate([x.reshape(-1, 16).T for x in idx]).astype(np.uint16)


def runs(offs, k):
    lists = np.stack([offs[16 * r : 16 * r + 16].T.reshape(-1) for r in range(8)]).astype(np.int64)
    return lists[np.arange(k) % 512 // 64]


def pack_weight(w):
    k, n = w.shape
    w = f64(np.asarray(w, np.float32).astype(ml_dtypes.bfloat16)).reshape(k // 32, 32, n)
    amax = np.abs(w).max(1)
    byte = np.clip(np.where(amax > 0, np.frexp(amax)[1] - 1 + 127 - 7, 1), 1, 254)
    scaled = (w * np.exp2(127.0 - byte)[:, None, :]).reshape(k, n).astype(np.float32)
    words = np.ascontiguousarray(scaled.reshape(k // 512, 128, 4, n).transpose(0, 1, 3, 2)).astype(ml_dtypes.float8_e4m3fn).view(np.uint8)
    return words, np.ascontiguousarray(byte.astype(np.uint8).reshape(k // 512, 16, n))


def unpack_weight(words, scales):
    g, p, n, _ = words.shape
    vals = np.ascontiguousarray(words).view(ml_dtypes.float8_e4m3fn).astype(np.float64) * np.repeat(np.exp2(scales.astype(np.float64) - 127.0), 8, axis=1)[..., None]
    return vals.transpose(0, 1, 3, 2).reshape(g * 512, n)


def sigmoid(v):
    return 1.0 / (1.0 + np.exp(-np.maximum(v, -700.0)))


K, T, S, H, C = 512, 2048, 256, 512, 512


def setup_inputs():
    n = np.random.standard_normal
    s = mx_kscale(K)[:, None]
    packed_xT = pack_weight(n((K, T)) * s)
    return {
        "x_words": packed_xT[0],
        "x_scales": packed_xT[1],
        "w1": (n((K, H)) / np.sqrt(K) / s).astype(np.float32),
        "sl": np.random.uniform(1.0, 2.0, (H, 1)).astype(np.float32),
        "th": (0.5 * n((H, 1))).astype(np.float32),
        "gs": (np.random.uniform(0.5, 1.5, (K, 1)) / s).astype(np.float32),
        "tau": np.random.uniform(0.3, 0.9, (C, 1)).astype(np.float32),
        "sl2": np.random.uniform(1.0, 2.0, (C, 1)).astype(np.float32),
        "th2": (0.5 * n((C, 1))).astype(np.float32),
        "offs": striped(np.random.permutation(T)[:S]),
        "n1": striped8(np.stack([np.random.permutation(S) for _ in range(8)])),
        "n2": striped8(np.stack([np.random.permutation(S) for _ in range(8)])),
        "ca": striped(np.random.permutation(T)[:C]),
        "cb": striped(np.random.permutation(T)[:C]),
        "cd": striped(np.random.permutation(T)[:C]),
        "n3": striped(np.random.permutation(S)),
        "n4": striped(np.random.permutation(S)),
        "n5": striped(np.random.permutation(S)),
        "n6": striped(np.random.permutation(S)),
    }


def reference(x_words, x_scales, w1, sl, th, gs, tau, sl2, th2, offs, n1, n2, ca, cb, cd, n3, n4, n5, n6):
    x_ca = unpack_weight(x_words, x_scales)[:, unstriped(ca)]
    xq = unpack_weight(x_words, x_scales)[:, unstriped(offs)]
    y = mxq(f64(w1), 0, "e4m3").T @ xq
    sg = sigmoid(f64(sl) * (y[np.arange(H)[:, None], runs(n1, H)] - f64(th)))
    st = y * sg
    z = f64(gs) * (st - (0.5 * (st[np.arange(H)[:, None], runs(n2, H)])))
    zq = mxq(z, 0, "e4m3")
    a = 0.0625 * (x_ca.T @ zq)
    x_cb = unpack_weight(x_words, x_scales)[:, unstriped(cb)]
    b = 0.0625 * (x_cb.T @ zq)
    top = b.max(axis=1, keepdims=True)
    ea = np.exp(f64(tau) * (b[:, unstriped(n3)] - top))
    m1 = (0.5 * (a - a[:, unstriped(n4)])) / (ea + 0.25)
    x_cd = unpack_weight(x_words, x_scales)[:, unstriped(cd)]
    q = 0.0625 * (x_cd.T @ zq)
    sg2 = sigmoid(f64(sl2) * (q[:, unstriped(n5)] - f64(th2)))
    return m1 * sg2 - (0.5 * m1[:, unstriped(n6)])

@@ -1,0 +1,198 @@
+from contextlib import ExitStack
+
+import concourse.mybir as mybir
+
+K, T, S, H, C = 512, 2048, 256, 512, 512
+FLOPS = 2 * K * S * (H + 3 * C)
+
+F32 = mybir.dt.float32
+BF16 = mybir.dt.bfloat16
+I32 = mybir.dt.int32
+U32 = mybir.dt.uint32
+U16 = mybir.dt.uint16
+U8 = mybir.dt.uint8
+FP8X4 = mybir.dt.float8_e4m3fn_x4
+ALU = mybir.AluOpType
+ACT = mybir.ActivationFunctionType
+
+P = 128
+PACK = 4
+WIN = 2 * S
+PIECE = 256
+KIB = 1024
+
+
+def tile_picked_tricdqxbgxbehp_none_p_kernel(tc, x_words, x_scales, w1, sl, th, gs, tau, sl2, th2, offs, n1, n2, ca, cb, cd, n3, n4, n5, n6, out):
+    nc = tc.nc
+    with ExitStack() as ctx:
+        keep = ctx.enter_context(tc.tile_pool(name="keep", bufs=1))
+        arena = ctx.enter_context(tc.tile_pool(name="arena", bufs=1))
+        psum = ctx.enter_context(tc.psum_pool(name="psum", bufs=1))
+
+        def new(name, shape, dtype, at=None):
+            if at is None:
+                return keep.tile(shape, dtype, name=name, align_bytes=64)
+            return arena.tile(shape, dtype, name=name, align_bytes=64, offset=at)
+
+        def load_list(name, src):
+            tile = keep.tile([P, src.shape[1]], U16, name=name)
+            nc.sync.dma_start(tile[:], src)
+            return tile
+
+        def load_rows(name, src, pattern, at=None):
+            tile = new(name, [P, PACK], F32, at)
+            with nc.allow_non_contiguous_dma(reason="one value a row"):
+                nc.sync.dma_start(tile[:], src.rearrange(pattern, p=P))
+            return tile
+
+        xs = new("xs", [P, T], U8)
+        nc.vector.memset(xs[:].bitcast(I32), 0)
+        l_offs = load_list("l_offs", offs)
+        for q in range(4):
+            nc.sync.dma_start(xs[32 * q : 32 * q + 4, :].bitcast(I32), x_scales[0, 4 * q : 4 * q + 4, :].bitcast(I32))
+        w_rows = w1.rearrange("(p j) c -> p j c", j=PACK)
+        w_raw = []
+        for h in range(2):
+            raw = new(f"w_raw{h}", [P, PACK, H // 2], F32)
+            nc.scalar.dma_start(raw[:], w_rows[:, :, h * (H // 2) : (h + 1) * (H // 2)])
+            w_raw.append(raw)
+        xw = new("xw", [P, T], U32)
+        nc.scalar.dma_start(xw[:].bitcast(I32), x_words[0].rearrange("p n t -> p (n t)").bitcast(I32))
+        l_cb = load_list("l_cb", cb)
+        l_ca = load_list("l_ca", ca)
+        l_n1 = load_list("l_n1", n1)
+        sl_t = load_rows("sl_t", sl, "(p t) o -> p (t o)")
+        th_t = load_rows("th_t", th, "(p t) o -> p (t o)")
+        gs_t = load_rows("gs_t", gs, "(p t) o -> p (t o)")
+        l_n2 = load_list("l_n2", n2)
+        l_cd = load_list("l_cd", cd)
+        l_n3 = load_list("l_n3", n3)
+        l_n4 = load_list("l_n4", n4)
+        l_n5 = load_list("l_n5", n5)
+        l_n6 = load_list("l_n6", n6)
+
+        def gather(name, window, lst, piece, dtype, at=None):
+            tile = new(name, [P, PIECE], dtype, at)
+            cols = PIECE // 16
+            nc.vector.tensor_copy(tile[:], window[:].indirect(lst[:, piece * cols : (piece + 1) * cols]))
+            return tile
+
+        xq_s = gather("xq_s", xs, l_offs, 0, U8)
+
+        w_bf = new("w_bf", [P, H * PACK], BF16, 24 * KIB)
+        w_dealt = w_bf[:].rearrange("p (t m j) -> p m j t", t=PACK, j=PACK)
+        for h in range(2):
+            nc.scalar.copy(w_dealt[:, 64 * h : 64 * (h + 1)], w_raw[h][:].rearrange("p j (m t) -> p m j t", t=PACK))
+        w_w = new("w_w", [P, H], U32, 0)
+        w_s = new("w_s", [P, H], U8)
+        nc.vector.quantize_mx(w_w[:].bitcast(FP8X4), w_s[:], w_bf[:])
+
+        xq_w = gather("xq_w", xw, l_offs, 0, U32)
+
+        bias1 = new("bias1", [P, PACK], F32)
+        nc.vector.scalar_tensor_tensor(bias1[:], sl_t[:], -1.0, th_t[:], ALU.mult, ALU.mult)
+        tau_t = load_rows("tau_t", tau, "(c p) o -> p (c o)", 24 * KIB)
+        sl2_t = load_rows("sl2_t", sl2, "(c p) o -> p (c o)", 24 * KIB + 64)
+        th2_t = load_rows("th2_t", th2, "(c p) o -> p (c o)", 24 * KIB + 128)
+
+        def product(dst, words, scales, rhs_w, rhs_s):
+            nc.tensor.matmul_mx(
+                out=dst, lhsT=words.bitcast(FP8X4), lhsT_scale=scales, rhs=rhs_w[:].bitcast(FP8X4), rhs_scale=rhs_s[:], start=True, stop=True
+            )
+
+        first = slice(0, S)
+        second = slice(S, 2 * S)
+        banks = [psum.tile([P, 2 * S], F32, name=f"bank{i}") for i in range(8)]
+        for t in range(PACK):
+            product(banks[t][:, first], w_w[:, P * t : P * (t + 1)], w_s[:, P * t : P * (t + 1)], xq_w, xq_s)
+
+        z = new("z", [P, PACK, S], F32)
+        y_at = [10 * KIB, 9 * KIB, 11 * KIB, 8 * KIB]
+        sg_at = [2 * KIB, 3 * KIB, 4 * KIB, None]
+        far_at = [5 * KIB, 13 * KIB, 14 * KIB, None]
+        for t in range(PACK):
+            col = slice(t, t + 1)
+            y_win = new(f"y_win{t}", [P, WIN], F32, y_at[t])
+            if t < 1:
+                nc.vector.tensor_copy(y_win[:, first], banks[t][:, first])
+            else:
+                nc.scalar.copy(y_win[:, first], banks[t][:, first])
+            sg = new(f"sg{t}", [P, S], F32, sg_at[t])
+            nc.scalar.activation(sg[:], y_win[:].indirect(l_n1[:]), ACT.Sigmoid, bias=bias1[:, col], scale=sl_t[:, col])
+            st_win = new(f"st_win{t}", [P, WIN], F32)
+            nc.vector.scalar_tensor_tensor(st_win[:, first], banks[t][:, first], gs_t[:, col], sg[:], ALU.mult, ALU.mult)
+            st_far = new(f"st_far{t}", [P, S], F32, far_at[t])
+            nc.scalar.activation(st_far[:], st_win[:].indirect(l_n2[:]), ACT.Copy)
+            nc.vector.scalar_tensor_tensor(z[:, t, :], st_far[:], -0.5, st_win[:, first], ALU.mult, ALU.add)
+        z_bf = new("z_bf", [P, S * PACK], BF16, 6 * KIB)
+        z_to = z_bf[:].rearrange("p (c i t) -> p c t i", i=4, t=PACK)
+        z_from = z[:].rearrange("p t (c i) -> p c t i", i=4)
+        nc.vector.tensor_copy(z_to[:, :36], z_from[:, :36])
+        nc.scalar.copy(z_to[:, 36:], z_from[:, 36:])
+        z_w = new("z_w", [P, S], U32)
+        z_s = new("z_s", [P, S], U8)
+        nc.vector.quantize_mx(z_w[:].bitcast(FP8X4), z_s[:], z_bf[:])
+
+        cb_s = [gather(f"cb_s{i}", xs, l_cb, i, U8) for i in range(2)]
+        ca_s = [gather(f"ca_s{i}", xs, l_ca, i, U8) for i in range(2)]
+        cb_w = [gather(f"cb_w{i}", xw, l_cb, i, U32, [0, 2 * KIB][i]) for i in range(2)]
+        ca_w = [gather(f"ca_w{i}", xw, l_ca, i, U32, [3 * KIB, 4 * KIB][i]) for i in range(2)]
+        cd_s = [gather(f"cd_s{i}", xs, l_cd, i, U8, [5 * KIB, 13 * KIB][i]) for i in range(2)]
+        cd_w = [gather(f"cd_w{i}", xw, l_cd, i, U32, [14 * KIB, 6 * KIB][i]) for i in range(2)]
+
+        def score(dst, words, scales, c):
+            cols = slice(P * (c % 2), P * (c % 2 + 1))
+            product(dst, words[c // 2][:, cols], scales[c // 2][:, cols], z_w, z_s)
+
+        for c in range(4):
+            score(banks[c][:, first], cb_w, cb_s, c)
+        for c in range(4):
+            score(banks[4 + c][:, first], ca_w, ca_s, c)
+
+        ea = new("ea", [P, 4, S], F32, 28 * KIB)
+        for c in range(4):
+            col = slice(c, c + 1)
+            b_win = new(f"b_win{c}", [P, WIN], F32, 16 * KIB if c == 3 else None)
+            top = new(f"top{c}", [P, 1], F32)
+            nc.vector.tensor_scalar(b_win[:, first], banks[c][:, first], 0.0625, None, ALU.mult, ALU.max, accum_out=top[:])
+            bias3 = new(f"bias3_{c}", [P, 1], F32)
+            nc.vector.tensor_scalar(bias3[:], top[:], tau_t[:, col], -1.0, ALU.mult, ALU.mult)
+            nc.scalar.activation(ea[:, c, :], b_win[:].indirect(l_n3[:]), ACT.Exp, bias=bias3[:], scale=tau_t[:, col])
+        root = new("root", [P, 4, S], F32, 17 * KIB)
+        inv = new("inv", [P, 4, S], F32)
+        for c in range(4):
+            nc.scalar.activation(root[:, c, :], ea[:, c, :], ACT.Abs_reciprocal_sqrt, bias=0.25)
+            nc.scalar.activation(inv[:, c, :], root[:, c, :], ACT.Square, scale=0.5)
+        for c in range(4):
+            score(banks[c][:, second], cd_w, cd_s, c)
+        bias2 = new("bias2", [P, PACK], F32)
+        nc.vector.scalar_tensor_tensor(bias2[:], sl2_t[:], -1.0, th2_t[:], ALU.mult, ALU.mult)
+        diffs = []
+        for c in range(4):
+            a_win = new(f"a_win{c}", [P, WIN], F32)
+            nc.vector.tensor_scalar(a_win[:, first], banks[4 + c][:, first], 0.0625, None, ALU.mult)
+            a_far = new(f"a_far{c}", [P, S], F32)
+            nc.vector.tensor_copy(a_far[:], a_win[:].indirect(l_n4[:]))
+            diff = new(f"diff{c}", [P, S], F32)
+            nc.vector.scalar_tensor_tensor(diff[:], banks[4 + c][:, first], -0.0625, a_far[:], ALU.mult, ALU.add)
+            diffs.append(diff)
+        sg2 = new("sg2", [P, 4, S], F32, 18 * KIB)
+        for c in range(4):
+            col = slice(c, c + 1)
+            q_win = new(f"q_win{c}", [P, WIN], F32, [27 * KIB, 29 * KIB, 31 * KIB, 16 * KIB][c])
+            nc.scalar.activation(q_win[:, first], banks[c][:, second], ACT.Copy, scale=0.0625)
+            nc.scalar.activation(sg2[:, c, :], q_win[:].indirect(l_n5[:]), ACT.Sigmoid, bias=bias2[:, col], scale=sl2_t[:, col])
+        m_wins, m_fars = [], []
+        for c in range(4):
+            m_win = new(f"m_win{c}", [P, WIN], F32)
+            nc.vector.tensor_tensor(m_win[:, first], diffs[c][:], inv[:, c, :], ALU.mult)
+            m_far = new(f"m_far{c}", [P, S], F32)
+            nc.vector.tensor_copy(m_far[:], m_win[:].indirect(l_n6[:]))
+            m_wins.append(m_win)
+            m_fars.append(m_far)
+        for c in range(4):
+            gated = new(f"gated{c}", [P, S], F32)
+            nc.vector.scalar_tensor_tensor(gated[:], m_wins[c][:, first], -2.0, sg2[:, c, :], ALU.mult, ALU.mult)
+            res = new(f"res{c}", [P, S], F32)
+            nc.vector.tensor_tensor(res[:], gated[:], m_fars[c][:], ALU.add)
+            nc.sync.dma_start(out[P * c : P * (c + 1), :], res[:])

@@ -45,25 +45,29 @@ def tile_picked_tricdqxbgxbehp_none_p_kernel(tc, x_words, x_scales, w1, sl, th, 
                 nc.sync.dma_start(tile[:], src.rearrange(pattern, p=P))
             return tile
 
+        xs_rows = new("xs_rows", [P, T // 4], I32)
         xs = new("xs", [P, T], U8)
         nc.vector.memset(xs[:].bitcast(I32), 0)
-        l_offs = load_list("l_offs", offs)
         for q in range(4):
-            nc.sync.dma_start(xs[32 * q : 32 * q + 4, :].bitcast(I32), x_scales[0, 4 * q : 4 * q + 4, :].bitcast(I32))
+            queue = nc.sync if q == 0 else nc.scalar
+            queue.dma_start(xs_rows[32 * q : 32 * q + 4, :], x_scales[0, 4 * q : 4 * q + 4, :].bitcast(I32))
+        l_offs = load_list("l_offs", offs)
+        l_cb = load_list("l_cb", cb)
         w_rows = w1.rearrange("(p j) c -> p j c", j=PACK)
         w_raw = []
         for h in range(2):
             raw = new(f"w_raw{h}", [P, PACK, H // 2], F32)
-            nc.scalar.dma_start(raw[:], w_rows[:, :, h * (H // 2) : (h + 1) * (H // 2)])
+            nc.sync.dma_start(raw[:], w_rows[:, :, h * (H // 2) : (h + 1) * (H // 2)])
             w_raw.append(raw)
-        xw = new("xw", [P, T], U32)
-        nc.scalar.dma_start(xw[:].bitcast(I32), x_words[0].rearrange("p n t -> p (n t)").bitcast(I32))
-        l_cb = load_list("l_cb", cb)
         l_ca = load_list("l_ca", ca)
-        l_n1 = load_list("l_n1", n1)
+        xw = new("xw", [P, T], U32)
+        nc.sync.dma_start(xw[:].bitcast(I32), x_words[0].rearrange("p n t -> p (n t)").bitcast(I32))
         sl_t = load_rows("sl_t", sl, "(p t) o -> p (t o)")
         th_t = load_rows("th_t", th, "(p t) o -> p (t o)")
+        l_n1 = load_list("l_n1", n1)
         gs_t = load_rows("gs_t", gs, "(p t) o -> p (t o)")
+        for q in range(4):
+            nc.vector.tensor_copy(xs[32 * q : 32 * q + 4, :].bitcast(I32), xs_rows[32 * q : 32 * q + 4, :])
         l_n2 = load_list("l_n2", n2)
         l_cd = load_list("l_cd", cd)
         l_n3 = load_list("l_n3", n3)
@@ -89,8 +93,12 @@ def tile_picked_tricdqxbgxbehp_none_p_kernel(tc, x_words, x_scales, w1, sl, th, 
 
         xq_w = gather("xq_w", xw, l_offs, 0, U32)
 
-        bias1 = new("bias1", [P, PACK], F32)
-        nc.vector.scalar_tensor_tensor(bias1[:], sl_t[:], -1.0, th_t[:], ALU.mult, ALU.mult)
+        def minus_product(name, left, right):
+            minus = new(name, [P, PACK], F32)
+            nc.vector.scalar_tensor_tensor(minus[:], left[:], -1.0, right[:], ALU.mult, ALU.mult)
+            return minus
+
+        bias1 = minus_product("bias1", sl_t, th_t)
         tau_t = load_rows("tau_t", tau, "(c p) o -> p (c o)", 24 * KIB)
         sl2_t = load_rows("sl2_t", sl2, "(c p) o -> p (c o)", 24 * KIB + 64)
         th2_t = load_rows("th2_t", th2, "(c p) o -> p (c o)", 24 * KIB + 128)
@@ -107,13 +115,14 @@ def tile_picked_tricdqxbgxbehp_none_p_kernel(tc, x_words, x_scales, w1, sl, th, 
             product(banks[t][:, first], w_w[:, P * t : P * (t + 1)], w_s[:, P * t : P * (t + 1)], xq_w, xq_s)
 
         z = new("z", [P, PACK, S], F32)
-        y_at = [10 * KIB, 9 * KIB, 11 * KIB, 8 * KIB]
-        sg_at = [2 * KIB, 3 * KIB, 4 * KIB, None]
-        far_at = [5 * KIB, 13 * KIB, 14 * KIB, None]
+        st_wins = []
+        y_at = [10 * KIB, None, 11 * KIB, 9 * KIB]
+        sg_at = [2 * KIB, 3 * KIB, 4 * KIB, 5 * KIB]
+        far_at = [9 * KIB, None, None, None]
         for t in range(PACK):
             col = slice(t, t + 1)
             y_win = new(f"y_win{t}", [P, WIN], F32, y_at[t])
-            if t < 1:
+            if t < 2:
                 nc.vector.tensor_copy(y_win[:, first], banks[t][:, first])
             else:
                 nc.scalar.copy(y_win[:, first], banks[t][:, first])
@@ -121,24 +130,31 @@ def tile_picked_tricdqxbgxbehp_none_p_kernel(tc, x_words, x_scales, w1, sl, th, 
             nc.scalar.activation(sg[:], y_win[:].indirect(l_n1[:]), ACT.Sigmoid, bias=bias1[:, col], scale=sl_t[:, col])
             st_win = new(f"st_win{t}", [P, WIN], F32)
             nc.vector.scalar_tensor_tensor(st_win[:, first], banks[t][:, first], gs_t[:, col], sg[:], ALU.mult, ALU.mult)
+            st_wins.append(st_win)
+        for t in range(PACK):
+            st_win = st_wins[t]
             st_far = new(f"st_far{t}", [P, S], F32, far_at[t])
             nc.scalar.activation(st_far[:], st_win[:].indirect(l_n2[:]), ACT.Copy)
             nc.vector.scalar_tensor_tensor(z[:, t, :], st_far[:], -0.5, st_win[:, first], ALU.mult, ALU.add)
         z_bf = new("z_bf", [P, S * PACK], BF16, 6 * KIB)
         z_to = z_bf[:].rearrange("p (c i t) -> p c t i", i=4, t=PACK)
         z_from = z[:].rearrange("p t (c i) -> p c t i", i=4)
-        nc.vector.tensor_copy(z_to[:, :36], z_from[:, :36])
-        nc.scalar.copy(z_to[:, 36:], z_from[:, 36:])
+        nc.vector.tensor_copy(z_to[:, :32], z_from[:, :32])
+        nc.scalar.copy(z_to[:, 32:], z_from[:, 32:])
         z_w = new("z_w", [P, S], U32)
         z_s = new("z_s", [P, S], U8)
         nc.vector.quantize_mx(z_w[:].bitcast(FP8X4), z_s[:], z_bf[:])
 
-        cb_s = [gather(f"cb_s{i}", xs, l_cb, i, U8) for i in range(2)]
-        ca_s = [gather(f"ca_s{i}", xs, l_ca, i, U8) for i in range(2)]
+        def gather_whole(name, lst):
+            tile = new(name, [P, 2, PIECE], U8)
+            nc.vector.tensor_copy(tile[:].rearrange("p i n -> p (i n)"), xs[:].indirect(lst[:]))
+            return [tile[:, i, :] for i in range(2)]
+
+        cb_s = gather_whole("cb_s", l_cb)
+        ca_s = gather_whole("ca_s", l_ca)
         cb_w = [gather(f"cb_w{i}", xw, l_cb, i, U32, [0, 2 * KIB][i]) for i in range(2)]
         ca_w = [gather(f"ca_w{i}", xw, l_ca, i, U32, [3 * KIB, 4 * KIB][i]) for i in range(2)]
-        cd_s = [gather(f"cd_s{i}", xs, l_cd, i, U8, [5 * KIB, 13 * KIB][i]) for i in range(2)]
-        cd_w = [gather(f"cd_w{i}", xw, l_cd, i, U32, [14 * KIB, 6 * KIB][i]) for i in range(2)]
+        cd_s = [gather(f"cd_s{i}", xs, l_cd, i, U8, [5 * KIB, 9 * KIB][i]) for i in range(2)]
 
         def score(dst, words, scales, c):
             cols = slice(P * (c % 2), P * (c % 2 + 1))
@@ -147,52 +163,59 @@ def tile_picked_tricdqxbgxbehp_none_p_kernel(tc, x_words, x_scales, w1, sl, th, 
         for c in range(4):
             score(banks[c][:, first], cb_w, cb_s, c)
         for c in range(4):
-            score(banks[4 + c][:, first], ca_w, ca_s, c)
+            score(banks[4 + c // 2][:, S * (c % 2) : S * (c % 2 + 1)], ca_w, ca_s, c)
 
         ea = new("ea", [P, 4, S], F32, 28 * KIB)
         for c in range(4):
             col = slice(c, c + 1)
-            b_win = new(f"b_win{c}", [P, WIN], F32, 16 * KIB if c == 3 else None)
+            b_win = new(f"b_win{c}", [P, WIN], F32, [34 * KIB, None, None, 16 * KIB][c])
             top = new(f"top{c}", [P, 1], F32)
             nc.vector.tensor_scalar(b_win[:, first], banks[c][:, first], 0.0625, None, ALU.mult, ALU.max, accum_out=top[:])
             bias3 = new(f"bias3_{c}", [P, 1], F32)
             nc.vector.tensor_scalar(bias3[:], top[:], tau_t[:, col], -1.0, ALU.mult, ALU.mult)
             nc.scalar.activation(ea[:, c, :], b_win[:].indirect(l_n3[:]), ACT.Exp, bias=bias3[:], scale=tau_t[:, col])
+        cd_w = [gather(f"cd_w{i}", xw, l_cd, i, U32, [6 * KIB, 34 * KIB][i]) for i in range(2)]
         root = new("root", [P, 4, S], F32, 17 * KIB)
         inv = new("inv", [P, 4, S], F32)
-        for c in range(4):
-            nc.scalar.activation(root[:, c, :], ea[:, c, :], ACT.Abs_reciprocal_sqrt, bias=0.25)
-            nc.scalar.activation(inv[:, c, :], root[:, c, :], ACT.Square, scale=0.5)
+        for h in range(2):
+            pair = slice(2 * h, 2 * h + 2)
+            nc.scalar.activation(root[:, pair, :], ea[:, pair, :], ACT.Abs_reciprocal_sqrt, bias=0.25)
+            nc.scalar.activation(inv[:, pair, :], root[:, pair, :], ACT.Square, scale=0.5)
         for c in range(4):
             score(banks[c][:, second], cd_w, cd_s, c)
-        bias2 = new("bias2", [P, PACK], F32)
-        nc.vector.scalar_tensor_tensor(bias2[:], sl2_t[:], -1.0, th2_t[:], ALU.mult, ALU.mult)
+        bias2 = minus_product("bias2", sl2_t, th2_t)
         diffs = []
-        for c in range(4):
-            a_win = new(f"a_win{c}", [P, WIN], F32)
-            nc.vector.tensor_scalar(a_win[:, first], banks[4 + c][:, first], 0.0625, None, ALU.mult)
-            a_far = new(f"a_far{c}", [P, S], F32)
-            nc.vector.tensor_copy(a_far[:], a_win[:].indirect(l_n4[:]))
-            diff = new(f"diff{c}", [P, S], F32)
-            nc.vector.scalar_tensor_tensor(diff[:], banks[4 + c][:, first], -0.0625, a_far[:], ALU.mult, ALU.add)
+        both = slice(0, 2 * S)
+        for h in range(2):
+            a_win = new(f"a_win{h}", [P, 3 * S], F32)
+            nc.vector.tensor_scalar(a_win[:, both], banks[4 + h][:], 0.0625, None, ALU.mult)
+            a_far = new(f"a_far{h}", [P, 2 * S], F32)
+            for i in range(2):
+                nc.vector.tensor_copy(a_far[:, S * i : S * (i + 1)], a_win[:, S * i : S * i + WIN].indirect(l_n4[:]))
+            diff = new(f"diff{h}", [P, 2 * S], F32)
+            nc.vector.scalar_tensor_tensor(diff[:], banks[4 + h][:], -0.0625, a_far[:], ALU.mult, ALU.add)
             diffs.append(diff)
         sg2 = new("sg2", [P, 4, S], F32, 18 * KIB)
         for c in range(4):
             col = slice(c, c + 1)
-            q_win = new(f"q_win{c}", [P, WIN], F32, [27 * KIB, 29 * KIB, 31 * KIB, 16 * KIB][c])
-            nc.scalar.activation(q_win[:, first], banks[c][:, second], ACT.Copy, scale=0.0625)
+            q_win = new(f"q_win{c}", [P, WIN], F32, [None, None, 29 * KIB, 31 * KIB][c])
+            if c < 2:
+                nc.vector.tensor_scalar(q_win[:, first], banks[c][:, second], 0.0625, None, ALU.mult)
+            else:
+                nc.scalar.activation(q_win[:, first], banks[c][:, second], ACT.Copy, scale=0.0625)
             nc.scalar.activation(sg2[:, c, :], q_win[:].indirect(l_n5[:]), ACT.Sigmoid, bias=bias2[:, col], scale=sl2_t[:, col])
         m_wins, m_fars = [], []
-        for c in range(4):
-            m_win = new(f"m_win{c}", [P, WIN], F32)
-            nc.vector.tensor_tensor(m_win[:, first], diffs[c][:], inv[:, c, :], ALU.mult)
-            m_far = new(f"m_far{c}", [P, S], F32)
-            nc.vector.tensor_copy(m_far[:], m_win[:].indirect(l_n6[:]))
-            m_wins.append(m_win)
-            m_fars.append(m_far)
+        for h in range(2):
+            m_win = new(f"m_win{h}", [P, 3 * S], F32)
+            nc.vector.tensor_tensor(m_win[:, both], diffs[h][:], inv[:, 2 * h : 2 * h + 2, :].rearrange("p c s -> p (c s)"), ALU.mult)
+            for i in range(2):
+                m_far = new(f"m_far{2 * h + i}", [P, S], F32)
+                nc.vector.tensor_copy(m_far[:], m_win[:, S * i : S * i + WIN].indirect(l_n6[:]))
+                m_wins.append(m_win[:, S * i : S * (i + 1)])
+                m_fars.append(m_far)
         for c in range(4):
             gated = new(f"gated{c}", [P, S], F32)
-            nc.vector.scalar_tensor_tensor(gated[:], m_wins[c][:, first], -2.0, sg2[:, c, :], ALU.mult, ALU.mult)
+            nc.vector.scalar_tensor_tensor(gated[:], m_wins[c], -2.0, sg2[:, c, :], ALU.mult, ALU.mult)
             res = new(f"res{c}", [P, S], F32)
             nc.vector.tensor_tensor(res[:], gated[:], m_fars[c][:], ALU.add)
             nc.sync.dma_start(out[P * c : P * (c + 1), :], res[:])

@@ -103,6 +103,11 @@ def tile_picked_tricdqxbgxbehp_none_p_kernel(tc, x_words, x_scales, w1, sl, th, 
         sl2_t = load_rows("sl2_t", sl2, "(c p) o -> p (c o)", 24 * KIB + 64)
         th2_t = load_rows("th2_t", th2, "(c p) o -> p (c o)", 24 * KIB + 128)
 
+        plus2 = new("plus2", [P, PACK], F32)
+        nc.gpsimd.tensor_tensor(plus2[:], sl2_t[:], th2_t[:], ALU.mult)
+        bias2 = new("bias2", [P, PACK], F32)
+        nc.gpsimd.tensor_scalar(bias2[:], plus2[:], -1.0, 0.0, ALU.mult, ALU.add)
+
         def product(dst, words, scales, rhs_w, rhs_s):
             nc.tensor.matmul_mx(
                 out=dst, lhsT=words.bitcast(FP8X4), lhsT_scale=scales, rhs=rhs_w[:].bitcast(FP8X4), rhs_scale=rhs_s[:], start=True, stop=True
@@ -116,13 +121,13 @@ def tile_picked_tricdqxbgxbehp_none_p_kernel(tc, x_words, x_scales, w1, sl, th, 
 
         z = new("z", [P, PACK, S], F32)
         st_wins = []
-        y_at = [10 * KIB, None, 11 * KIB, 9 * KIB]
+        y_at = [10 * KIB, None, None, 9 * KIB]
         sg_at = [2 * KIB, 3 * KIB, 4 * KIB, 5 * KIB]
         far_at = [9 * KIB, None, None, None]
         for t in range(PACK):
             col = slice(t, t + 1)
             y_win = new(f"y_win{t}", [P, WIN], F32, y_at[t])
-            if t < 2:
+            if t < 3:
                 nc.vector.tensor_copy(y_win[:, first], banks[t][:, first])
             else:
                 nc.scalar.copy(y_win[:, first], banks[t][:, first])
@@ -172,7 +177,7 @@ def tile_picked_tricdqxbgxbehp_none_p_kernel(tc, x_words, x_scales, w1, sl, th, 
             top = new(f"top{c}", [P, 1], F32)
             nc.vector.tensor_scalar(b_win[:, first], banks[c][:, first], 0.0625, None, ALU.mult, ALU.max, accum_out=top[:])
             bias3 = new(f"bias3_{c}", [P, 1], F32)
-            nc.vector.tensor_scalar(bias3[:], top[:], tau_t[:, col], -1.0, ALU.mult, ALU.mult)
+            (nc.vector if c < 2 else nc.gpsimd).tensor_scalar(bias3[:], top[:], tau_t[:, col], -1.0, ALU.mult, ALU.mult)
             nc.scalar.activation(ea[:, c, :], b_win[:].indirect(l_n3[:]), ACT.Exp, bias=bias3[:], scale=tau_t[:, col])
         cd_w = [gather(f"cd_w{i}", xw, l_cd, i, U32, [6 * KIB, 34 * KIB][i]) for i in range(2)]
         root = new("root", [P, 4, S], F32, 17 * KIB)
@@ -183,39 +188,53 @@ def tile_picked_tricdqxbgxbehp_none_p_kernel(tc, x_words, x_scales, w1, sl, th, 
             nc.scalar.activation(inv[:, pair, :], root[:, pair, :], ACT.Square, scale=0.5)
         for c in range(4):
             score(banks[c][:, second], cd_w, cd_s, c)
-        bias2 = minus_product("bias2", sl2_t, th2_t)
-        diffs = []
+        diffs, q_wins = [], []
         both = slice(0, 2 * S)
+        a_wins = []
         for h in range(2):
             a_win = new(f"a_win{h}", [P, 3 * S], F32)
             nc.vector.tensor_scalar(a_win[:, both], banks[4 + h][:], 0.0625, None, ALU.mult)
+            if h == 1:
+                for c in range(1):
+                    q_win = new(f"q_win{c}", [P, WIN], F32)
+                    nc.vector.tensor_scalar(q_win[:, first], banks[c][:, second], 0.0625, None, ALU.mult)
+                    q_wins.append(q_win)
             a_far = new(f"a_far{h}", [P, 2 * S], F32)
             for i in range(2):
                 nc.vector.tensor_copy(a_far[:, S * i : S * (i + 1)], a_win[:, S * i : S * i + WIN].indirect(l_n4[:]))
             diff = new(f"diff{h}", [P, 2 * S], F32)
-            nc.vector.scalar_tensor_tensor(diff[:], banks[4 + h][:], -0.0625, a_far[:], ALU.mult, ALU.add)
+            nc.gpsimd.tensor_tensor(diff[:], a_far[:], a_win[:, both], ALU.subtract)
             diffs.append(diff)
+        for c in range(1, 4):
+            q_win = new(f"q_win{c}", [P, WIN], F32)
+            nc.vector.tensor_scalar(q_win[:, first], banks[c][:, second], 0.0625, None, ALU.mult)
+            q_wins.append(q_win)
+        def spans(c):
+            return [(0, S)]
+
         sg2 = new("sg2", [P, 4, S], F32, 18 * KIB)
         for c in range(4):
             col = slice(c, c + 1)
-            q_win = new(f"q_win{c}", [P, WIN], F32, [None, None, 29 * KIB, 31 * KIB][c])
-            if c < 2:
-                nc.vector.tensor_scalar(q_win[:, first], banks[c][:, second], 0.0625, None, ALU.mult)
-            else:
-                nc.scalar.activation(q_win[:, first], banks[c][:, second], ACT.Copy, scale=0.0625)
-            nc.scalar.activation(sg2[:, c, :], q_win[:].indirect(l_n5[:]), ACT.Sigmoid, bias=bias2[:, col], scale=sl2_t[:, col])
+            for a, b in spans(c):
+                nc.scalar.activation(
+                    sg2[:, c, a:b], q_wins[c][:].indirect(l_n5[:, a // 16 : b // 16]), ACT.Sigmoid, bias=bias2[:, col], scale=sl2_t[:, col]
+                )
         m_wins, m_fars = [], []
         for h in range(2):
             m_win = new(f"m_win{h}", [P, 3 * S], F32)
             nc.vector.tensor_tensor(m_win[:, both], diffs[h][:], inv[:, 2 * h : 2 * h + 2, :].rearrange("p c s -> p (c s)"), ALU.mult)
             for i in range(2):
                 m_far = new(f"m_far{2 * h + i}", [P, S], F32)
-                nc.vector.tensor_copy(m_far[:], m_win[:, S * i : S * i + WIN].indirect(l_n6[:]))
+                if 2 * h + i < 3:
+                    nc.vector.tensor_copy(m_far[:], m_win[:, S * i : S * i + WIN].indirect(l_n6[:]))
+                else:
+                    nc.scalar.activation(m_far[:], m_win[:, S * i : S * i + WIN].indirect(l_n6[:]), ACT.Copy)
                 m_wins.append(m_win[:, S * i : S * (i + 1)])
                 m_fars.append(m_far)
         for c in range(4):
             gated = new(f"gated{c}", [P, S], F32)
-            nc.vector.scalar_tensor_tensor(gated[:], m_wins[c], -2.0, sg2[:, c, :], ALU.mult, ALU.mult)
             res = new(f"res{c}", [P, S], F32)
-            nc.vector.tensor_tensor(res[:], gated[:], m_fars[c][:], ALU.add)
-            nc.sync.dma_start(out[P * c : P * (c + 1), :], res[:])
+            for a, b in spans(c):
+                nc.vector.scalar_tensor_tensor(gated[:, a:b], m_wins[c][:, a:b], -2.0, sg2[:, c, a:b], ALU.mult, ALU.mult)
+                nc.vector.tensor_tensor(res[:, a:b], gated[:, a:b], m_fars[c][:, a:b], ALU.add)
+                nc.sync.dma_start(out[P * c : P * (c + 1), a:b], res[:, a:b])

@@ -167,48 +167,51 @@ def tile_picked_tricdqxbgxbehp_none_p_kernel(tc, x_words, x_scales, w1, sl, th, 
 
         for c in range(4):
             score(banks[c][:, first], cb_w, cb_s, c)
-        for c in range(4):
-            score(banks[4 + c // 2][:, S * (c % 2) : S * (c % 2 + 1)], ca_w, ca_s, c)
+        for c in range(2):
+            score(banks[4][:, S * c : S * (c + 1)], ca_w, ca_s, c)
 
         ea = new("ea", [P, 4, S], F32, 28 * KIB)
         for c in range(4):
             col = slice(c, c + 1)
-            b_win = new(f"b_win{c}", [P, WIN], F32, [34 * KIB, None, None, 16 * KIB][c])
+            b_win = new(f"b_win{c}", [P, WIN], F32, [34 * KIB, 36 * KIB, 38 * KIB, 16 * KIB][c])
             top = new(f"top{c}", [P, 1], F32)
             nc.vector.tensor_scalar(b_win[:, first], banks[c][:, first], 0.0625, None, ALU.mult, ALU.max, accum_out=top[:])
             bias3 = new(f"bias3_{c}", [P, 1], F32)
             (nc.vector if c < 2 else nc.gpsimd).tensor_scalar(bias3[:], top[:], tau_t[:, col], -1.0, ALU.mult, ALU.mult)
             nc.scalar.activation(ea[:, c, :], b_win[:].indirect(l_n3[:]), ACT.Exp, bias=bias3[:], scale=tau_t[:, col])
-        cd_w = [gather(f"cd_w{i}", xw, l_cd, i, U32, [6 * KIB, 34 * KIB][i]) for i in range(2)]
+        cd_w = [gather("cd_w0", xw, l_cd, 0, U32, 6 * KIB)]
         root = new("root", [P, 4, S], F32, 17 * KIB)
         inv = new("inv", [P, 4, S], F32)
         for h in range(2):
             pair = slice(2 * h, 2 * h + 2)
             nc.scalar.activation(root[:, pair, :], ea[:, pair, :], ACT.Abs_reciprocal_sqrt, bias=0.25)
             nc.scalar.activation(inv[:, pair, :], root[:, pair, :], ACT.Square, scale=0.5)
-        for c in range(4):
-            score(banks[c][:, second], cd_w, cd_s, c)
         diffs, q_wins = [], []
         both = slice(0, 2 * S)
-        a_wins = []
         for h in range(2):
             a_win = new(f"a_win{h}", [P, 3 * S], F32)
-            nc.vector.tensor_scalar(a_win[:, both], banks[4 + h][:], 0.0625, None, ALU.mult)
-            if h == 1:
-                for c in range(1):
-                    q_win = new(f"q_win{c}", [P, WIN], F32)
+            nc.vector.tensor_scalar(a_win[:, both], banks[4][:], 0.0625, None, ALU.mult)
+            if h == 0:
+                for c in range(2, 4):
+                    score(banks[4][:, S * (c - 2) : S * (c - 1)], ca_w, ca_s, c)
+                cd_w.append(gather("cd_w1", xw, l_cd, 1, U32, 34 * KIB))
+                for c in range(4):
+                    score(banks[c][:, second], cd_w, cd_s, c)
+            else:
+                for c in range(4):
+                    q_win = new(f"q_win{c}", [P, WIN], F32, [15 * KIB, 38 * KIB, 36 * KIB, None][c])
                     nc.vector.tensor_scalar(q_win[:, first], banks[c][:, second], 0.0625, None, ALU.mult)
                     q_wins.append(q_win)
             a_far = new(f"a_far{h}", [P, 2 * S], F32)
             for i in range(2):
                 nc.vector.tensor_copy(a_far[:, S * i : S * (i + 1)], a_win[:, S * i : S * i + WIN].indirect(l_n4[:]))
             diff = new(f"diff{h}", [P, 2 * S], F32)
-            nc.gpsimd.tensor_tensor(diff[:], a_far[:], a_win[:, both], ALU.subtract)
+            if h == 0:
+                nc.gpsimd.tensor_tensor(diff[:], a_far[:], a_win[:, both], ALU.subtract)
+            else:
+                nc.vector.scalar_tensor_tensor(diff[:], banks[4][:], -0.0625, a_far[:], ALU.mult, ALU.add)
             diffs.append(diff)
-        for c in range(1, 4):
-            q_win = new(f"q_win{c}", [P, WIN], F32)
-            nc.vector.tensor_scalar(q_win[:, first], banks[c][:, second], 0.0625, None, ALU.mult)
-            q_wins.append(q_win)
+
         def spans(c):
             return [(0, S)]
 

from contextlib import ExitStack

import concourse.mybir as mybir

K, T, S, H, C = 512, 2048, 256, 512, 512
FLOPS = 2 * K * S * (H + 3 * C)

F32 = mybir.dt.float32
BF16 = mybir.dt.bfloat16
I32 = mybir.dt.int32
U32 = mybir.dt.uint32
U16 = mybir.dt.uint16
U8 = mybir.dt.uint8
FP8X4 = mybir.dt.float8_e4m3fn_x4
ALU = mybir.AluOpType
ACT = mybir.ActivationFunctionType

P = 128
PACK = 4
WIN = 2 * S
PIECE = 256
KIB = 1024


def tile_picked_tricdqxbgxbehp_none_p_kernel(tc, x_words, x_scales, w1, sl, th, gs, tau, sl2, th2, offs, n1, n2, ca, cb, cd, n3, n4, n5, n6, out):
    nc = tc.nc
    with ExitStack() as ctx:
        keep = ctx.enter_context(tc.tile_pool(name="keep", bufs=1))
        arena = ctx.enter_context(tc.tile_pool(name="arena", bufs=1))
        psum = ctx.enter_context(tc.psum_pool(name="psum", bufs=1))

        def new(name, shape, dtype, at=None):
            if at is None:
                return keep.tile(shape, dtype, name=name, align_bytes=64)
            return arena.tile(shape, dtype, name=name, align_bytes=64, offset=at)

        def load_list(name, src):
            tile = keep.tile([P, src.shape[1]], U16, name=name)
            nc.sync.dma_start(tile[:], src)
            return tile

        def load_rows(name, src, pattern, at=None):
            tile = new(name, [P, PACK], F32, at)
            with nc.allow_non_contiguous_dma(reason="one value a row"):
                nc.sync.dma_start(tile[:], src.rearrange(pattern, p=P))
            return tile

        xs_rows = new("xs_rows", [P, T // 4], I32)
        xs = new("xs", [P, T], U8)
        nc.vector.memset(xs[:].bitcast(I32), 0)
        for q in range(4):
            queue = nc.sync if q == 0 else nc.scalar
            queue.dma_start(xs_rows[32 * q : 32 * q + 4, :], x_scales[0, 4 * q : 4 * q + 4, :].bitcast(I32))
        l_offs = load_list("l_offs", offs)
        l_cb = load_list("l_cb", cb)
        w_rows = w1.rearrange("(p j) c -> p j c", j=PACK)
        w_raw = []
        for h in range(2):
            raw = new(f"w_raw{h}", [P, PACK, H // 2], F32)
            nc.sync.dma_start(raw[:], w_rows[:, :, h * (H // 2) : (h + 1) * (H // 2)])
            w_raw.append(raw)
        l_ca = load_list("l_ca", ca)
        xw = new("xw", [P, T], U32)
        nc.sync.dma_start(xw[:].bitcast(I32), x_words[0].rearrange("p n t -> p (n t)").bitcast(I32))
        sl_t = load_rows("sl_t", sl, "(p t) o -> p (t o)")
        th_t = load_rows("th_t", th, "(p t) o -> p (t o)")
        l_n1 = load_list("l_n1", n1)
        gs_t = load_rows("gs_t", gs, "(p t) o -> p (t o)")
        for q in range(4):
            nc.vector.tensor_copy(xs[32 * q : 32 * q + 4, :].bitcast(I32), xs_rows[32 * q : 32 * q + 4, :])
        l_n2 = load_list("l_n2", n2)
        l_cd = load_list("l_cd", cd)
        l_n3 = load_list("l_n3", n3)
        l_n4 = load_list("l_n4", n4)
        l_n5 = load_list("l_n5", n5)
        l_n6 = load_list("l_n6", n6)

        def gather(name, window, lst, piece, dtype, at=None):
            tile = new(name, [P, PIECE], dtype, at)
            cols = PIECE // 16
            nc.vector.tensor_copy(tile[:], window[:].indirect(lst[:, piece * cols : (piece + 1) * cols]))
            return tile

        xq_s = gather("xq_s", xs, l_offs, 0, U8)

        w_bf = new("w_bf", [P, H * PACK], BF16, 24 * KIB)
        w_dealt = w_bf[:].rearrange("p (t m j) -> p m j t", t=PACK, j=PACK)
        for h in range(2):
            nc.scalar.copy(w_dealt[:, 64 * h : 64 * (h + 1)], w_raw[h][:].rearrange("p j (m t) -> p m j t", t=PACK))
        w_w = new("w_w", [P, H], U32, 0)
        w_s = new("w_s", [P, H], U8)
        nc.vector.quantize_mx(w_w[:].bitcast(FP8X4), w_s[:], w_bf[:])

        xq_w = gather("xq_w", xw, l_offs, 0, U32)

        def minus_product(name, left, right):
            minus = new(name, [P, PACK], F32)
            nc.vector.scalar_tensor_tensor(minus[:], left[:], -1.0, right[:], ALU.mult, ALU.mult)
            return minus

        bias1 = minus_product("bias1", sl_t, th_t)
        tau_t = load_rows("tau_t", tau, "(c p) o -> p (c o)", 24 * KIB)
        sl2_t = load_rows("sl2_t", sl2, "(c p) o -> p (c o)", 24 * KIB + 64)
        th2_t = load_rows("th2_t", th2, "(c p) o -> p (c o)", 24 * KIB + 128)

        plus2 = new("plus2", [P, PACK], F32)
        nc.gpsimd.tensor_tensor(plus2[:], sl2_t[:], th2_t[:], ALU.mult)
        bias2 = new("bias2", [P, PACK], F32)
        nc.gpsimd.tensor_scalar(bias2[:], plus2[:], -1.0, 0.0, ALU.mult, ALU.add)

        def product(dst, words, scales, rhs_w, rhs_s):
            nc.tensor.matmul_mx(
                out=dst, lhsT=words.bitcast(FP8X4), lhsT_scale=scales, rhs=rhs_w[:].bitcast(FP8X4), rhs_scale=rhs_s[:], start=True, stop=True
            )

        first = slice(0, S)
        second = slice(S, 2 * S)
        banks = [psum.tile([P, 2 * S], F32, name=f"bank{i}") for i in range(8)]
        for t in range(PACK):
            product(banks[t][:, first], w_w[:, P * t : P * (t + 1)], w_s[:, P * t : P * (t + 1)], xq_w, xq_s)

        z = new("z", [P, PACK, S], F32)
        st_wins = []
        y_at = [10 * KIB, None, None, 9 * KIB]
        sg_at = [2 * KIB, 3 * KIB, 4 * KIB, 5 * KIB]
        far_at = [9 * KIB, None, None, None]
        for t in range(PACK):
            col = slice(t, t + 1)
            y_win = new(f"y_win{t}", [P, WIN], F32, y_at[t])
            if t < 3:
                nc.vector.tensor_copy(y_win[:, first], banks[t][:, first])
            else:
                nc.scalar.copy(y_win[:, first], banks[t][:, first])
            sg = new(f"sg{t}", [P, S], F32, sg_at[t])
            nc.scalar.activation(sg[:], y_win[:].indirect(l_n1[:]), ACT.Sigmoid, bias=bias1[:, col], scale=sl_t[:, col])
            st_win = new(f"st_win{t}", [P, WIN], F32)
            nc.vector.scalar_tensor_tensor(st_win[:, first], banks[t][:, first], gs_t[:, col], sg[:], ALU.mult, ALU.mult)
            st_wins.append(st_win)
        for t in range(PACK):
            st_win = st_wins[t]
            st_far = new(f"st_far{t}", [P, S], F32, far_at[t])
            nc.scalar.activation(st_far[:], st_win[:].indirect(l_n2[:]), ACT.Copy)
            nc.vector.scalar_tensor_tensor(z[:, t, :], st_far[:], -0.5, st_win[:, first], ALU.mult, ALU.add)
        z_bf = new("z_bf", [P, S * PACK], BF16, 6 * KIB)
        z_to = z_bf[:].rearrange("p (c i t) -> p c t i", i=4, t=PACK)
        z_from = z[:].rearrange("p t (c i) -> p c t i", i=4)
        nc.vector.tensor_copy(z_to[:, :32], z_from[:, :32])
        nc.scalar.copy(z_to[:, 32:], z_from[:, 32:])
        z_w = new("z_w", [P, S], U32)
        z_s = new("z_s", [P, S], U8)
        nc.vector.quantize_mx(z_w[:].bitcast(FP8X4), z_s[:], z_bf[:])

        def gather_whole(name, lst):
            tile = new(name, [P, 2, PIECE], U8)
            nc.vector.tensor_copy(tile[:].rearrange("p i n -> p (i n)"), xs[:].indirect(lst[:]))
            return [tile[:, i, :] for i in range(2)]

        cb_s = gather_whole("cb_s", l_cb)
        ca_s = gather_whole("ca_s", l_ca)
        cb_w = [gather(f"cb_w{i}", xw, l_cb, i, U32, [0, 2 * KIB][i]) for i in range(2)]
        ca_w = [gather(f"ca_w{i}", xw, l_ca, i, U32, [3 * KIB, 4 * KIB][i]) for i in range(2)]
        cd_s = [gather(f"cd_s{i}", xs, l_cd, i, U8, [5 * KIB, 9 * KIB][i]) for i in range(2)]

        def score(dst, words, scales, c):
            cols = slice(P * (c % 2), P * (c % 2 + 1))
            product(dst, words[c // 2][:, cols], scales[c // 2][:, cols], z_w, z_s)

        for c in range(4):
            score(banks[c][:, first], cb_w, cb_s, c)
        for c in range(2):
            score(banks[4][:, S * c : S * (c + 1)], ca_w, ca_s, c)

        ea = new("ea", [P, 4, S], F32, 28 * KIB)
        for c in range(4):
            col = slice(c, c + 1)
            b_win = new(f"b_win{c}", [P, WIN], F32, [34 * KIB, 36 * KIB, 38 * KIB, 16 * KIB][c])
            top = new(f"top{c}", [P, 1], F32)
            nc.vector.tensor_scalar(b_win[:, first], banks[c][:, first], 0.0625, None, ALU.mult, ALU.max, accum_out=top[:])
            bias3 = new(f"bias3_{c}", [P, 1], F32)
            (nc.vector if c < 2 else nc.gpsimd).tensor_scalar(bias3[:], top[:], tau_t[:, col], -1.0, ALU.mult, ALU.mult)
            nc.scalar.activation(ea[:, c, :], b_win[:].indirect(l_n3[:]), ACT.Exp, bias=bias3[:], scale=tau_t[:, col])
        cd_w = [gather("cd_w0", xw, l_cd, 0, U32, 6 * KIB)]
        root = new("root", [P, 4, S], F32, 17 * KIB)
        inv = new("inv", [P, 4, S], F32)
        for h in range(2):
            pair = slice(2 * h, 2 * h + 2)
            nc.scalar.activation(root[:, pair, :], ea[:, pair, :], ACT.Abs_reciprocal_sqrt, bias=0.25)
            nc.scalar.activation(inv[:, pair, :], root[:, pair, :], ACT.Square, scale=0.5)
        diffs, q_wins = [], []
        both = slice(0, 2 * S)
        for h in range(2):
            a_win = new(f"a_win{h}", [P, 3 * S], F32)
            nc.vector.tensor_scalar(a_win[:, both], banks[4][:], 0.0625, None, ALU.mult)
            if h == 0:
                for c in range(2, 4):
                    score(banks[4][:, S * (c - 2) : S * (c - 1)], ca_w, ca_s, c)
                cd_w.append(gather("cd_w1", xw, l_cd, 1, U32, 34 * KIB))
                for c in range(4):
                    score(banks[c][:, second], cd_w, cd_s, c)
            else:
                for c in range(4):
                    q_win = new(f"q_win{c}", [P, WIN], F32, [15 * KIB, 38 * KIB, 36 * KIB, None][c])
                    nc.vector.tensor_scalar(q_win[:, first], banks[c][:, second], 0.0625, None, ALU.mult)
                    q_wins.append(q_win)
            a_far = new(f"a_far{h}", [P, 2 * S], F32)
            for i in range(2):
                nc.vector.tensor_copy(a_far[:, S * i : S * (i + 1)], a_win[:, S * i : S * i + WIN].indirect(l_n4[:]))
            diff = new(f"diff{h}", [P, 2 * S], F32)
            if h == 0:
                nc.gpsimd.tensor_tensor(diff[:], a_far[:], a_win[:, both], ALU.subtract)
            else:
                nc.vector.scalar_tensor_tensor(diff[:], banks[4][:], -0.0625, a_far[:], ALU.mult, ALU.add)
            diffs.append(diff)

        def spans(c):
            return [(0, S)]

        sg2 = new("sg2", [P, 4, S], F32, 18 * KIB)
        for c in range(4):
            col = slice(c, c + 1)
            for a, b in spans(c):
                nc.scalar.activation(
                    sg2[:, c, a:b], q_wins[c][:].indirect(l_n5[:, a // 16 : b // 16]), ACT.Sigmoid, bias=bias2[:, col], scale=sl2_t[:, col]
                )
        m_wins, m_fars = [], []
        for h in range(2):
            m_win = new(f"m_win{h}", [P, 3 * S], F32)
            nc.vector.tensor_tensor(m_win[:, both], diffs[h][:], inv[:, 2 * h : 2 * h + 2, :].rearrange("p c s -> p (c s)"), ALU.mult)
            for i in range(2):
                m_far = new(f"m_far{2 * h + i}", [P, S], F32)
                if 2 * h + i < 3:
                    nc.vector.tensor_copy(m_far[:], m_win[:, S * i : S * i + WIN].indirect(l_n6[:]))
                else:
                    nc.scalar.activation(m_far[:], m_win[:, S * i : S * i + WIN].indirect(l_n6[:]), ACT.Copy)
                m_wins.append(m_win[:, S * i : S * (i + 1)])
                m_fars.append(m_far)
        for c in range(4):
            gated = new(f"gated{c}", [P, S], F32)
            res = new(f"res{c}", [P, S], F32)
            for a, b in spans(c):
                nc.vector.scalar_tensor_tensor(gated[:, a:b], m_wins[c][:, a:b], -2.0, sg2[:, c, a:b], ALU.mult, ALU.mult)
                nc.vector.tensor_tensor(res[:, a:b], gated[:, a:b], m_fars[c][:, a:b], ALU.add)
                nc.sync.dma_start(out[P * c : P * (c + 1), a:b], res[:, a:b])
